import numpy as np, ml_dtypes
CORES = [3,7,11,15,131,135,139,143]
N = 8
DEG, TK = 4, 256
MASK = [[0,4,5,7],[0,1,3,6],[2,3,4,5],[1,3,5,7],[2,3,4,6],[1,5,6,7],[1,3,4,6],[2,3,5,7]]
def setup_inputs(rng):
    return {"x": rng.standard_normal((N, 128, TK), dtype=np.float32).astype(ml_dtypes.bfloat16), "w": rng.standard_normal((N, 128, DEG * 128), dtype=np.float32).astype(ml_dtypes.bfloat16)}
def setup_inputs_big(rng):
    d = setup_inputs(rng)
    for k in ("x", "w"): d[k] = (d[k].astype(np.float32) * 1024.0).astype(d[k].dtype)
    return d
def setup_inputs_small(rng):
    d = setup_inputs(rng)
    for k in ("x", "w"): d[k] = (d[k].astype(np.float32) * (1 / 1024.0)).astype(d[k].dtype)
    return d
def setup_inputs_apart(rng):
    d = setup_inputs(rng)
    f = (10.0 ** rng.permutation(np.linspace(-1.5, 1.5, N))).astype(np.float32).reshape(N, 1, 1)
    for k in ("x", "w"): d[k] = (d[k].astype(np.float32) * f).astype(d[k].dtype)
    return d
def reference(x, w):
    X, W = x.astype(np.float64), w.astype(np.float64)
    y = np.zeros((N, 128, TK))
    for r in range(N):
        for i, j in enumerate(MASK[r]):
            y[r] += W[r][:, 128 * i:128 * i + 128].T @ X[j]
    return {"y": y.astype(ml_dtypes.bfloat16 if x.dtype != np.float64 else np.float64)}

from concourse.bass import DstId, RemoteDMATransfer

N, DEG, TK, TM = 8, 4, 256, 128
RELAY = False

SCRATCH = {
    "xin": ("sbuf", [128, DEG * TK], "bfloat16"),
    "wsb": ("sbuf", [128, DEG * TM], "bfloat16"),
    "ysb": ("sbuf", [128, TK], "bfloat16"),
    "acc": ("psum", [128, 512], "float32"),
}
SEMAPHORES = ["xl", "wl", "sent", "mm", "cp", "st"] + ["a%d" % j for j in range(N)]


def _same_chip(topo, a, b):
    return topo.host(a) == topo.host(b) and topo.chip(a) == topo.chip(b)


def _links(topo, a, b):
    if _same_chip(topo, a, b):
        return 0
    return 1 if (topo.mates(a, b) or topo.same_plane(a, b)) else 2


def _count(mask):
    return bin(mask).count("1")


def _routes(T, topo):
    cores, mask = T.cores, T.tables["MASK"]
    out = []
    for j in range(N):
        s = cores[j]
        dests = [r for r in range(N) if r != j and j in mask[r]]
        near = [r for r in dests if _same_chip(topo, s, cores[r])]
        far = [r for r in dests if r not in near]
        fwd = []
        if RELAY:
            keep = []
            for r in far:
                group = [q for q in far if _same_chip(topo, cores[q], cores[r])]
                head = sorted(group, key=lambda q: (topo.die(cores[q]) != topo.die(s), q))[0]
                if r == head:
                    keep.append(r)
                else:
                    fwd.append((head, r))
            far = keep
        heads = [f for f, _ in fwd]
        far.sort(key=lambda r: (r not in heads, -_links(topo, s, cores[r]), topo.mates(s, cores[r]), r))
        out.append({"far": far, "near": near, "fwd": fwd})
    return out


def _masks(T, topo, j, routes):
    cores = T.cores
    s = cores[j]
    chipmate = [c for c in cores if c != s and _same_chip(topo, s, c)][0]
    away = [c for c in cores if not _same_chip(topo, s, c)]
    m_far = topo.mask(s, away[0])
    for c in away:
        m_far &= topo.mask(s, c)
    m_near = topo.mask(s, chipmate) & ~m_far
    return m_far, m_near


def rank_program(g, core, T, topo):
    rank = T.rank_of(core)
    if rank is None:
        return
    cores, mask, sem = T.cores, T.tables["MASK"], T.sem
    routes = _routes(T, topo)
    row = mask[rank]

    def slot(r, j):
        i = mask[r].index(j)
        return T.xin[:, TK * i:TK * (i + 1)]

    def send(j, dests, engines):
        ids = []
        for r in dests:
            rid, pid = topo.addr(cores[r], core)
            ids.append(DstId(rid=rid, pnc=pid))
        g.remote_dma_fused(
            [RemoteDMATransfer(dst_ids=ids, dma_engine_mask=engines, remote_sem=sem["a%d" % j],
                               srcs=[slot(rank, j)], dsts=[slot(r, j) for r in dests], alu_op=0)],
            local_sem=sem.sent)
        return _count(engines)

    g.sync.dma_start(slot(rank, rank), T.x[:, :]).then_inc(sem.xl, 16)
    g.sync.dma_start(T.wsb[:, :], T.w[:, :]).then_inc(sem.wl, 16)

    m_far, m_near = _masks(T, topo, rank, routes)
    mine = routes[rank]
    sent = 0
    g.wait_ge(sem.xl, 16)
    if mine["far"]:
        sent += send(rank, mine["far"], m_far)
    if mine["near"]:
        sent += send(rank, mine["near"], m_near)

    arrive = {}
    for j in row:
        if j == rank:
            continue
        f_far, f_near = _masks(T, topo, j, routes)
        rt = routes[j]
        if rank in rt["far"]:
            arrive[j] = (_count(f_far), 1.0 + rt["far"].index(rank))
        elif rank in rt["near"]:
            arrive[j] = (_count(f_near), 1.5)
        else:
            f = [a for a, b in rt["fwd"] if b == rank][0]
            arrive[j] = (_count(_masks(T, topo, f, routes)[1]), 4.0 + rt["far"].index(f))

    duties = [(j, r) for j in range(N) for f, r in routes[j]["fwd"] if f == rank]
    duties.sort(key=lambda d: arrive[d[0]][1])
    for j, r in duties:
        g.wait_ge(sem["a%d" % j], arrive[j][0])
        sent += send(j, [r], m_near)
    g.wait_ge(sem.sent, sent)

    order = [rank] + sorted(arrive, key=lambda j: arrive[j][1])
    g.tensor.wait_ge(sem.xl, 16)
    g.tensor.wait_ge(sem.wl, 16)
    for n, j in enumerate(order):
        if j != rank:
            g.tensor.wait_ge(sem["a%d" % j], arrive[j][0])
        i = row.index(j)
        mm = g.tensor.matmul(T.acc[:, 0:TK], T.wsb[:, TM * i:TM * (i + 1)], slot(rank, j),
                             start=(n == 0), stop=(n == DEG - 1))
    mm.then_inc(sem.mm, 1)

    g.vector.wait_ge(sem.mm, 1)
    g.vector.tensor_copy(T.ysb[:, :], T.acc[:, 0:TK]).then_inc(sem.cp, 1)
    g.sync.wait_ge(sem.cp, 1)
    g.sync.dma_start(T.y[:, :], T.ysb[:, :]).then_inc(sem.st, 16)
    g.sync.wait_ge(sem.st, 16)
